import numpy as np, ml_dtypes
CORES = [31,71,111]
N = 3
KT, HT, TK = 1, 4, 128
def setup_inputs(rng):
    w = (rng.standard_normal((128, KT * HT * 128), dtype=np.float32) / 8).astype(ml_dtypes.bfloat16)
    return {"x": rng.standard_normal((N, 128, KT * TK), dtype=np.float32).astype(ml_dtypes.bfloat16), "w": np.broadcast_to(w, (N,) + w.shape).copy()}
def setup_inputs_big(rng):
    d = setup_inputs(rng)
    for k in ("x", "w"): d[k] = (d[k].astype(np.float32) * 1024.0).astype(d[k].dtype)
    return d
def setup_inputs_small(rng):
    d = setup_inputs(rng)
    for k in ("x", "w"): d[k] = (d[k].astype(np.float32) * (1 / 1024.0)).astype(d[k].dtype)
    return d
def setup_inputs_apart(rng):
    d = setup_inputs(rng)
    f = (10.0 ** rng.permutation(np.linspace(-1.5, 1.5, N))).astype(np.float32).reshape(N, 1, 1)
    for k in ("x",): d[k] = (d[k].astype(np.float32) * f).astype(d[k].dtype)
    return d
def reference(x, w):
    X, W = x.astype(np.float64), w.astype(np.float64)
    def hidden(r):
        return np.stack([np.maximum(sum(W[r][:, 128 * (HT * t + u):128 * (HT * t + u) + 128].T @ X[r][:, TK * t:TK * t + TK] for t in range(KT)), 0.0) for u in range(HT)])
    h = [hidden(r) for r in range(N)]
    y = np.stack([sum(h[(r - 1) % N][u].T @ h[r][u] for u in range(HT)) for r in range(N)])
    return {"y": y.astype(ml_dtypes.bfloat16)}

from concourse.mybir import AluOpType

HT = 4
TK = 128

SCRATCH = {
    "xs": ("sbuf", [128, TK], "bfloat16"),
    "ws": ("sbuf", [128, HT * 128], "bfloat16"),
    "xp": ("sbuf", [128, TK], "bfloat16"),
    "zero": ("sbuf", [128, HT * TK], "float32"),
    "h": ("sbuf", [128, HT * TK], "bfloat16"),
    "hp": ("sbuf", [128, HT * TK], "bfloat16"),
    "ys": ("sbuf", [128, TK], "bfloat16"),
    "ph": ("psum", [128, 512], "float32"),
    "pp0": ("psum", [128, 512], "float32"),
    "pp1": ("psum", [128, 512], "float32"),
    "pp2": ("psum", [128, 512], "float32"),
    "pp3": ("psum", [128, 512], "float32"),
    "py": ("psum", [128, 512], "float32"),
}
SEMAPHORES = ["xl", "wl", "zs", "sent", "arrived", "mh", "rh",
              "mp0", "mp1", "mp2", "mp3", "rp0", "rp1", "rp2", "rp3", "my", "cy", "stored"]


def engines_of(mask):
    return [e for e in range(16) if (mask >> e) & 1]


def rank_program(g, core, T, topo):
    rank = T.rank_of(core)
    if rank is None:
        return
    n = len(T.cores)
    nxt = T.cores[(rank + 1) % n]
    prv = T.cores[(rank - 1) % n]
    if not topo.may_write(core, nxt):
        raise ValueError("rank core cannot reach its successor directly")
    S = T.sem

    g.sync.dma_start(T.xs[:], T.x[:]).then_inc(S.xl, 16)
    g.sync.dma_start(T.ws[:], T.w[:]).then_inc(S.wl, 16)
    g.vector.memset(T.zero[:], 0.0).then_inc(S.zs, 1)

    out_mask = topo.mask(core, nxt)
    in_count = len(engines_of(topo.mask(prv, core)))
    rid, pid, _ = topo.addr(nxt)
    g.wait_ge(S.xl, 16)
    g.remote_dma(out_ap=T.xp[:], in_ap=T.xs[:], remote_sem=S.arrived, local_sem=S.sent,
                 pid=pid, routing_id=rid, dma_engine_mask=out_mask)

    te, ve = g.tensor, g.vector
    te.wait_ge(S.xl, 16)
    te.wait_ge(S.wl, 16)
    for u in range(HT):
        te.matmul(T.ph[:, u * TK:(u + 1) * TK], T.ws[:, u * 128:(u + 1) * 128], T.xs[:], True, True).then_inc(S.mh, 1)
    ve.wait_ge(S.zs, 1)
    ve.wait_ge(S.mh, HT)
    ve.tensor_tensor(T.h[:], T.ph[:], T.zero[:], AluOpType.max).then_inc(S.rh, 1)

    te.wait_ge(S.arrived, in_count)
    for u in range(HT):
        te.matmul(T["pp%d" % u][:, 0:TK], T.ws[:, u * 128:(u + 1) * 128], T.xp[:], True, True).then_inc(S["mp%d" % u], 1)
    for u in range(HT):
        ve.wait_ge(S["mp%d" % u], 1)
        ve.tensor_tensor(T.hp[:, u * TK:(u + 1) * TK], T["pp%d" % u][:, 0:TK], T.zero[:, 0:TK],
                         AluOpType.max).then_inc(S["rp%d" % u], 1)
    te.wait_ge(S.rh, 1)
    for u in range(HT):
        te.wait_ge(S["rp%d" % u], 1)
        mm = te.matmul(T.py[:, 0:TK], T.hp[:, u * TK:(u + 1) * TK], T.h[:, u * TK:(u + 1) * TK], u == 0, u == HT - 1)
        if u == HT - 1:
            mm.then_inc(S.my, 1)
    ve.wait_ge(S.my, 1)
    ve.tensor_copy(T.ys[:], T.py[:, 0:TK]).then_inc(S.cy, 1)

    g.sync.wait_ge(S.cy, 1)
    g.sync.dma_start(T.y[:], T.ys[:]).then_inc(S.stored, 16)
    g.sync.wait_ge(S.stored, 16)
    g.wait_ge(S.sent, len(engines_of(out_mask)))
